import numpy as np
import ml_dtypes


def mxq(x, axis, fmt="e4m3"):
    dtype, down = {"e4m3": (ml_dtypes.float8_e4m3fn, 7), "e5m2": (ml_dtypes.float8_e5m2, 14)}[fmt]
    v = np.moveaxis(np.asarray(x, np.float32).astype(ml_dtypes.bfloat16).astype(np.float64), axis, -1)
    blocks = v.reshape(v.shape[:-1] + (-1, 32))
    amax = np.abs(blocks).max(-1, keepdims=True)
    byte = np.maximum(np.where(amax > 0, np.frexp(amax)[1] - 1 + 127, 0) - down, 1)
    scale = np.exp2(byte - 127.0)
    codes = (blocks / scale).astype(np.float32).astype(dtype).astype(np.float64)
    return np.moveaxis((codes * scale).reshape(v.shape), -1, axis)


WIDE = False


def mx_kscale(k):
    if not WIDE:
        return np.ones(k)
    levels = np.array([10, -10, 5, -5, 0])
    if k % 512:
        return np.exp2(np.random.permutation(np.resize(levels, k // 32))).repeat(32)
    a = np.empty((k // 512, 16))
    for p in range(k // 512):
        a[p, :8] = np.random.permutation(np.resize(levels, 8))
        for g in range(8):
            far = levels[np.abs(levels - a[p, g]) >= 10]
            a[p, g + 8] = far[np.random.randint(len(far))]
    return np.exp2(a.ravel()).repeat(32)


def f64(x):
    return np.asarray(x).astype(np.float64)


def striped(idx):
    return np.tile(idx.reshape(-1, 16).T, (8, 1)).astype(np.uint16)


def unstriped(offs):
    return offs[:16].T.reshape(-1).astype(np.int64)


E2M1 = np.array([0.0, 0.5, 1.0, 1.5, 2.0, 3.0, 4.0, 6.0, -0.0, -0.5, -1.0, -1.5, -2.0, -3.0, -4.0, -6.0])


def pack_weight(w, fmt):
    k, n = w.shape
    w = f64(np.asarray(w, np.float32).astype(ml_dtypes.bfloat16)).reshape(k // 32, 32, n)
    amax = np.abs(w).max(1)
    if fmt == "e4m3":
        byte = np.frexp(amax)[1] - 1 + 127 - 7
    else:
        mant, ex = np.frexp(amax / 6.0)
        byte = np.where(mant > 0.5, ex, ex - 1) + 127
    byte = np.clip(np.where(amax > 0, byte, 1), 1, 254)
    scaled = (w * np.exp2(127.0 - byte)[:, None, :]).reshape(k, n).astype(np.float32)
    by_word = np.ascontiguousarray(scaled.reshape(k // 512, 128, 4, n).transpose(0, 1, 3, 2))
    if fmt == "e4m3":
        words = by_word.astype(ml_dtypes.float8_e4m3fn).view(np.uint8)
    else:
        c = by_word.astype(ml_dtypes.float4_e2m1fn).view(np.uint8) & 0xF
        words = (c[..., 0::2] | (c[..., 1::2] << 4)).reshape(k // 512, 128, 2 * n)
    return np.ascontiguousarray(words), np.ascontiguousarray(byte.astype(np.uint8).reshape(k // 512, 16, n))


def unpack_weight(words, scales, fmt):
    g, _, n = scales.shape
    words = np.ascontiguousarray(words).reshape(g, 128, n, -1)
    if fmt == "e4m3":
        vals = words.view(ml_dtypes.float8_e4m3fn).astype(np.float64)
    else:
        nib = np.empty((g, 128, n, 4), np.uint8)
        nib[..., 0::2] = words & 0xF
        nib[..., 1::2] = words >> 4
        vals = E2M1[nib]
    vals = vals * np.repeat(np.exp2(scales.astype(np.float64) - 127.0), 8, axis=1)[..., None]
    return vals.transpose(0, 1, 3, 2).reshape(g * 512, n)


def gelu(v):
    return 0.5 * v * (1.0 + np.tanh(np.sqrt(2.0 / np.pi) * (v + 0.044715 * v**3)))


K, H, T, S, S2, T3, P = 1024, 1024, 4096, 1024, 512, 2048, 512


def setup_inputs():
    n = np.random.standard_normal
    s = mx_kscale(K)[:, None]
    u = mx_kscale(H)[:, None]
    d = {}
    d["tab_words"], d["tab_scales"] = pack_weight(n((K, T)) * s, "e4m3")
    d["offs"] = striped(np.random.permutation(T)[:S])
    d["w4_words"], d["w4_scales"] = pack_weight(n((K, H)) / K**0.5 / s * u.T, "e2m1")
    d["w1"] = (0.8 * n((K, H)) / K**0.5 / s * np.sqrt(u).T).astype(np.float32)
    d["tab2_words"], d["tab2_scales"] = pack_weight(n((H, T3)) / H**0.5 / u, "e4m3")
    d["offs2"] = striped(np.random.permutation(T3)[:S2])
    d["pos1"] = striped(np.random.permutation(S)[:P])
    d["pos2"] = striped(np.random.permutation(S)[:P])
    d["allow"] = np.random.uniform(0.3, 1.7, (S2, P)).astype(np.float32)
    return d


def reference(tab_words, tab_scales, offs, w4_words, w4_scales, w1,
              tab2_words, tab2_scales, offs2, pos1, pos2, allow):
    v = unpack_weight(tab_words, tab_scales, "e4m3")[:, unstriped(offs)]
    v2 = unpack_weight(tab2_words, tab2_scales, "e4m3")[:, unstriped(offs2)]
    w4 = unpack_weight(w4_words, w4_scales, "e2m1")
    first = mxq(f64(w1), 0, "e4m3").T @ v
    second = w4.T @ v
    h = second - np.square(first)
    e = v2.T @ mxq(h, 0, "e4m3")
    gap = np.abs(e[:, unstriped(pos1)] - e[:, unstriped(pos2)])
    return f64(allow) * np.exp(-gap)

@@ -1,0 +1,283 @@
+from contextlib import ExitStack
+
+import concourse.mybir as mybir
+
+K, H, T, S, S2, T3, NP = 1024, 1024, 4096, 1024, 512, 2048, 512
+FLOPS = 2 * (2 * K * H * S + H * S2 * S)
+
+F32 = mybir.dt.float32
+BF16 = mybir.dt.bfloat16
+I32 = mybir.dt.int32
+U32 = mybir.dt.uint32
+U16 = mybir.dt.uint16
+U8 = mybir.dt.uint8
+FP8X4 = mybir.dt.float8_e4m3fn_x4
+FP4X4 = mybir.dt.float4_e2m1fn_x4
+ACT = mybir.ActivationFunctionType
+ALU = mybir.AluOpType
+
+P = 128
+PACK = 4
+KP = P * PACK
+BANK = 512
+UNIT = 256
+
+
+def tile_list_banquet_neighbour_scores_kernel(
+    tc, tab_words, tab_scales, offs, w4_words, w4_scales, w1, tab2_words, tab2_scales, offs2, pos1, pos2, allow, out
+):
+    nc = tc.nc
+    with ExitStack() as ctx:
+        keep = ctx.enter_context(tc.tile_pool(name="keep", bufs=1))
+        ring = ctx.enter_context(tc.tile_pool(name="ring", bufs=2))
+        psum = ctx.enter_context(tc.psum_pool(name="psum", bufs=1))
+
+        def held(shape, dtype, name):
+            return keep.tile(shape, dtype, name=name, align_bytes=64)
+
+        def bank(i):
+            return psum.tile([P, BANK], F32, name="bank%d" % i)
+
+        def load_list(src, name):
+            t = keep.tile([P, src.shape[1]], U16, name=name)
+            nc.sync.dma_start(t[:], src)
+            return t
+
+        def words(src, a):
+            return src[a].rearrange("p t i -> p (t i)").bitcast(I32)
+
+        def load_packed_scales(queue, tile, src):
+            for q in range(4):
+                queue.dma_start(tile[32 * q : 32 * q + 8, :].bitcast(I32), src[:, 4 * q : 4 * q + 4, :].bitcast(I32))
+
+        def load_w1(a, b):
+            t = ring.tile([P, PACK, KP], F32, name="w1_raw", align_bytes=64)
+            nc.sync.dma_start(t[:], w1[a * KP : (a + 1) * KP, b * KP : (b + 1) * KP].rearrange("(p j) c -> p j c", j=PACK))
+            return t
+
+        tab_sc = held([P, T], U8, "tab_sc")
+        w4_sc_raw = held([P, 2, H], U8, "w4_sc_raw")
+        v_sc1 = held([P, S], U8, "v_sc1")
+        nc.vector.memset(tab_sc[:].bitcast(I32), 0)
+        nc.vector.memset(w4_sc_raw[:].bitcast(I32), 0)
+        nc.vector.memset(v_sc1[:].bitcast(I32), 0)
+        tab2_sc = held([P, T3], U8, "tab2_sc")
+        nc.gpsimd.memset(tab2_sc[:].bitcast(I32), 0)
+        load_packed_scales(nc.gpsimd, tab2_sc, tab2_scales)
+        warm_in = held([P, 16], F32, "warm_in")
+        warm_out = held([P, 16], F32, "warm_out")
+        nc.vector.memset(warm_in[:], 0.0)
+        nc.scalar.activation(warm_out[:], warm_in[:], ACT.Exp)
+
+        tab = [held([P, T], I32, "tab0")]
+        nc.sync.dma_start(tab[0][:, : T // 2], words(tab_words, 0)[:, : T // 2])
+        idx = load_list(offs, "idx")
+        load_packed_scales(nc.sync, tab_sc, tab_scales)
+        nc.sync.dma_start(tab[0][:, T // 2 :], words(tab_words, 0)[:, T // 2 :])
+        w1_raw = {(0, 0): load_w1(0, 0)}
+        w4_raw = held([P, 2, 2 * H], U8, "w4_raw")
+        nc.sync.dma_start(w4_raw[:].bitcast(I32), w4_words.rearrange("a p c -> p a c").bitcast(I32))
+        w1_raw[1, 0] = load_w1(1, 0)
+        idx2 = load_list(offs2, "idx2")
+        for q in range(4):
+            nc.sync.dma_start(
+                w4_sc_raw[32 * q : 32 * q + 4].bitcast(I32),
+                w4_scales[:, 4 * q : 4 * q + 4, :].rearrange("a r c -> r a c").bitcast(I32),
+            )
+        tab.append(held([P, T], I32, "tab1"))
+        nc.sync.dma_start(tab[1][:], words(tab_words, 1))
+
+        v_sc = held([P, S], U8, "v_sc")
+        v = {}
+        w1_q, w1_sc, w4_q = {}, {}, {}
+
+        def gather_v(a, half):
+            t = held([P, BANK], U32, "v%d%d" % (a, half))
+            nc.vector.tensor_copy(t[:], tab[a][:].bitcast(U32).indirect(idx[:, 32 * half : 32 * (half + 1)]))
+            v[a, half] = t
+
+        def quantise_w1(a, b):
+            grouped = ring.tile([P, PACK * KP], BF16, name="w1_bf", align_bytes=64)
+            nc.scalar.copy(
+                grouped[:].rearrange("p (t m j) -> p m t j", t=PACK, j=PACK),
+                w1_raw[a, b][:].rearrange("p j (m t) -> p m t j", t=PACK),
+            )
+            codes = held([P, KP], U32, "w1_q%d%d" % (a, b))
+            scales = held([P, KP], U8, "w1_sc%d%d" % (a, b))
+            nc.vector.quantize_mx(codes[:].bitcast(FP8X4), scales[:], grouped[:])
+            w1_q[a, b], w1_sc[a, b] = codes, scales
+
+        def deal_w4(b):
+            t = held([P, 2, 2 * KP], U8, "w4_q%d" % b)
+            nc.vector.tensor_copy(
+                t[:].bitcast(U16).rearrange("p a (t m) -> p a t m", t=PACK),
+                w4_raw[:, :, 2 * KP * b : 2 * KP * (b + 1)].bitcast(U16).rearrange("p a (m t) -> p a t m", t=PACK),
+            )
+            w4_q[b] = t
+
+        nc.vector.tensor_copy(v_sc[:], tab_sc[:].indirect(idx[:]))
+        for q in range(4):
+            nc.gpsimd.dma_start(v_sc1[32 * q : 32 * q + 4, :].bitcast(I32), v_sc[32 * q + 4 : 32 * q + 8, :].bitcast(I32))
+        gather_v(0, 0)
+        quantise_w1(0, 0)
+        gather_v(0, 1)
+        w1_raw[0, 1] = load_w1(0, 1)
+        w4_sc = held([P, 2 * H], U8, "w4_sc")
+        nc.vector.tensor_copy(
+            w4_sc[:].rearrange("p (g t m) -> p g t m", t=PACK, m=P),
+            w4_sc_raw[:].rearrange("p a (b m t) -> p (a b) t m", t=PACK, m=P),
+        )
+        deal_w4(0)
+        quantise_w1(1, 0)
+        w1_raw[1, 1] = load_w1(1, 1)
+        p1 = load_list(pos1, "p1")
+        p2 = load_list(pos2, "p2")
+        deal_w4(1)
+        v2_sc = held([P, S2], U8, "v2_sc")
+        nc.vector.tensor_copy(v2_sc[:], tab2_sc[:].indirect(idx2[:]))
+        gather_v(1, 0)
+
+        h_q, h_sc = {}, {}
+        for b in range(2):
+            for half in range(2):
+                h_q[b, half] = held([P, BANK], U32, "h_q%d%d" % (b, half))
+                h_sc[b, half] = held([P, BANK], U8, "h_sc%d%d" % (b, half))
+
+        def stage1(u):
+            b, jq = divmod(u, S // UNIT)
+            half, c0 = divmod(jq * UNIT, BANK)
+            j0 = jq * UNIT
+            base = 4 * (u % 2)
+            first = [bank(base), bank(base + 1)]
+            second = [bank(base + 2), bank(base + 3)]
+
+            def first_pass(pair, a):
+                for s in range(2):
+                    t = 2 * pair + s
+                    nc.tensor.matmul_mx(
+                        first[pair][:, s * UNIT : (s + 1) * UNIT],
+                        lhsT=w1_q[a, b][:, t * P : (t + 1) * P].bitcast(FP8X4),
+                        lhsT_scale=w1_sc[a, b][:, t * P : (t + 1) * P],
+                        rhs=v[a, half][:, c0 : c0 + UNIT].bitcast(FP8X4),
+                        rhs_scale=v_sc[4 * a : P, j0 : j0 + UNIT],
+                        start=(a == 0 and s == 0),
+                        stop=(a == 1 and s == 1),
+                    )
+
+            def second_pass(g, a):
+                for t in range(PACK):
+                    sc0 = (2 * a + b) * KP + t * P
+                    nc.tensor.matmul_mx(
+                        second[g][:, t * P : (t + 1) * P],
+                        lhsT=w4_q[b][:, a, 2 * t * P : 2 * (t + 1) * P].bitcast(FP4X4),
+                        lhsT_scale=w4_sc[:, sc0 : sc0 + P],
+                        rhs=v[a, half][:, c0 + g * P : c0 + (g + 1) * P].bitcast(FP8X4),
+                        rhs_scale=(v_sc, v_sc1)[a][:, j0 + g * P : j0 + (g + 1) * P],
+                        start=(a == 0 and t == 0),
+                        stop=(a == 1 and t == PACK - 1),
+                    )
+
+            for one_pass in (first_pass, second_pass):
+                for i in range(2):
+                    for a in range(2):
+                        one_pass(i, a)
+            sq = ring.tile([P, 2, UNIT, 2], F32, name="sq", align_bytes=64)
+            for pair in range(2):
+                nc.scalar.activation(sq[:, pair], first[pair][:].rearrange("p (s j) -> p j s", s=2), ACT.Square)
+            h_bf = ring.tile([P, UNIT * PACK], BF16, name="h_bf", align_bytes=64)
+            for g in range(2):
+                nc.vector.tensor_tensor(
+                    h_bf[:, g * BANK : (g + 1) * BANK].rearrange("p (j r s) -> p j r s", r=2, s=2),
+                    second[g][:].rearrange("p (r s j) -> p j r s", r=2, s=2),
+                    sq[:, :, g * P : (g + 1) * P, :].rearrange("p r j s -> p j r s"),
+                    ALU.subtract,
+                )
+            step = P if u == 7 else UNIT
+            for c in range(0, UNIT, step):
+                cols = slice(c0 + c, c0 + c + step)
+                nc.vector.quantize_mx(
+                    h_q[b, half][:, cols].bitcast(FP8X4), h_sc[b, half][:, cols], h_bf[:, PACK * c : PACK * (c + step)]
+                )
+
+        v2 = []
+
+        def gather_v2(b):
+            t = held([P, S2], U32, "v2_%d" % b)
+            nc.vector.tensor_copy(t[:], tab2[:, b * T3 : (b + 1) * T3].bitcast(U32).indirect(idx2[:]))
+            v2.append(t)
+
+        stage1(0)
+        gather_v(1, 1)
+        tab2 = held([P, 2 * T3], I32, "tab1")
+        for b in range(2):
+            nc.sync.dma_start(tab2[:, b * T3 : (b + 1) * T3], words(tab2_words, b))
+        stage1(1)
+        quantise_w1(0, 1)
+        allow_sb = ring.tile([P, S2 // P, NP], F32, name="w1_raw", align_bytes=64)
+        nc.sync.dma_start(allow_sb[:], allow.rearrange("(m p) n -> p m n", p=P))
+        stage1(2)
+        quantise_w1(1, 1)
+        stage1(3)
+        stage1(4)
+        gather_v2(0)
+        stage1(5)
+        gather_v2(1)
+        stage1(6)
+        stage1(7)
+
+        e = [held([P, S], F32, "e%d" % m) for m in range(S2 // P)]
+
+        def scores(m, half):
+            acc = bank(4 * half + m)
+            pieces = [(0, 0, BANK), (1, 0, BANK)]
+            if half == 1:
+                pieces = [(0, 0, BANK), (1, 0, UNIT), (1, UNIT, UNIT + P), (1, UNIT + P, BANK)]
+            for i, (b, lo, hi) in enumerate(pieces):
+                nc.tensor.matmul_mx(
+                    acc[:, lo:hi],
+                    lhsT=v2[b][:, m * P : (m + 1) * P].bitcast(FP8X4),
+                    lhsT_scale=v2_sc[4 * b : P, m * P : (m + 1) * P],
+                    rhs=h_q[b, half][:, lo:hi].bitcast(FP8X4),
+                    rhs_scale=h_sc[b, half][:, lo:hi],
+                    start=(i == 0),
+                    stop=(i == len(pieces) - 1),
+                )
+            nc.scalar.copy(e[m][:, half * BANK : (half + 1) * BANK], acc[:])
+
+        for m in range(S2 // P):
+            for half in range(2):
+                scores(m, half)
+
+        guest, agree = {}, {}
+
+        def pick_guest(m):
+            guest[m] = held([P, NP], F32, "guest%d" % m)
+            nc.vector.tensor_copy(guest[m][:], e[m][:].indirect(p1[:]))
+
+        def compare(m, lo, hi):
+            gap = held([P, hi - lo], F32, "gap%d_%d" % (m, lo))
+            nc.vector.tensor_tensor(gap[:], e[m][:].indirect(p2[:, lo // 16 : hi // 16]), guest[m][:, lo:hi], ALU.subtract)
+            dist = held([P, hi - lo], F32, "dist%d_%d" % (m, lo))
+            nc.scalar.activation(dist[:], gap[:], ACT.Abs)
+            agree[m, lo] = held([P, hi - lo], F32, "agree%d_%d" % (m, lo))
+            nc.scalar.activation(agree[m, lo][:], dist[:], ACT.Exp, scale=-1.0)
+
+        def finish(m, lo, hi):
+            res = held([P, hi - lo], F32, "res%d_%d" % (m, lo))
+            nc.vector.tensor_tensor(res[:], agree[m, lo][:], allow_sb[:, m, lo:hi], ALU.mult)
+            nc.sync.dma_start(out[m * P : (m + 1) * P, lo:hi], res[:])
+
+        pick_guest(0)
+        pick_guest(1)
+        compare(0, 0, NP)
+        pick_guest(2)
+        compare(1, 0, NP)
+        finish(0, 0, NP)
+        pick_guest(3)
+        compare(2, 0, NP)
+        finish(1, 0, NP)
+        compare(3, 0, NP // 2)
+        compare(3, NP // 2, NP)
+        finish(2, 0, NP)
+        finish(3, 0, NP // 2)
+        finish(3, NP // 2, NP)

@@ -46,9 +46,9 @@ def tile_list_banquet_neighbour_scores_kernel(
         def words(src, a):
             return src[a].rearrange("p t i -> p (t i)").bitcast(I32)
 
-        def load_packed_scales(queue, tile, src):
+        def load_packed_scales(queue, tile, src, row):
             for q in range(4):
-                queue.dma_start(tile[32 * q : 32 * q + 8, :].bitcast(I32), src[:, 4 * q : 4 * q + 4, :].bitcast(I32))
+                queue.dma_start(tile[32 * q + row : 32 * q + row + 8, :].bitcast(I32), src[:, 4 * q : 4 * q + 4, :].bitcast(I32))
 
         def load_w1(a, b):
             t = ring.tile([P, PACK, KP], F32, name="w1_raw", align_bytes=64)
@@ -60,10 +60,10 @@ def tile_list_banquet_neighbour_scores_kernel(
         v_sc1 = held([P, S], U8, "v_sc1")
         nc.vector.memset(tab_sc[:].bitcast(I32), 0)
         nc.vector.memset(w4_sc_raw[:].bitcast(I32), 0)
-        nc.vector.memset(v_sc1[:].bitcast(I32), 0)
         tab2_sc = held([P, T3], U8, "tab2_sc")
         nc.gpsimd.memset(tab2_sc[:].bitcast(I32), 0)
-        load_packed_scales(nc.gpsimd, tab2_sc, tab2_scales)
+        nc.vector.memset(v_sc1[:].bitcast(I32), 0)
+        load_packed_scales(nc.gpsimd, tab2_sc, tab2_scales, 8)
         warm_in = held([P, 16], F32, "warm_in")
         warm_out = held([P, 16], F32, "warm_out")
         nc.vector.memset(warm_in[:], 0.0)
@@ -72,20 +72,18 @@ def tile_list_banquet_neighbour_scores_kernel(
         tab = [held([P, T], I32, "tab0")]
         nc.sync.dma_start(tab[0][:, : T // 2], words(tab_words, 0)[:, : T // 2])
         idx = load_list(offs, "idx")
-        load_packed_scales(nc.sync, tab_sc, tab_scales)
+        load_packed_scales(nc.sync, tab_sc, tab_scales, 0)
         nc.sync.dma_start(tab[0][:, T // 2 :], words(tab_words, 0)[:, T // 2 :])
         w1_raw = {(0, 0): load_w1(0, 0)}
         w4_raw = held([P, 2, 2 * H], U8, "w4_raw")
         nc.sync.dma_start(w4_raw[:].bitcast(I32), w4_words.rearrange("a p c -> p a c").bitcast(I32))
-        w1_raw[1, 0] = load_w1(1, 0)
-        idx2 = load_list(offs2, "idx2")
         for q in range(4):
             nc.sync.dma_start(
                 w4_sc_raw[32 * q : 32 * q + 4].bitcast(I32),
                 w4_scales[:, 4 * q : 4 * q + 4, :].rearrange("a r c -> r a c").bitcast(I32),
             )
-        tab.append(held([P, T], I32, "tab1"))
-        nc.sync.dma_start(tab[1][:], words(tab_words, 1))
+        w1_raw[1, 0] = load_w1(1, 0)
+        idx2 = load_list(offs2, "idx2")
 
         v_sc = held([P, S], U8, "v_sc")
         v = {}
@@ -98,10 +96,11 @@ def tile_list_banquet_neighbour_scores_kernel(
 
         def quantise_w1(a, b):
             grouped = ring.tile([P, PACK * KP], BF16, name="w1_bf", align_bytes=64)
-            nc.scalar.copy(
-                grouped[:].rearrange("p (t m j) -> p m t j", t=PACK, j=PACK),
-                w1_raw[a, b][:].rearrange("p j (m t) -> p m t j", t=PACK),
-            )
+            for m0 in range(0, P, 32):
+                nc.scalar.copy(
+                    grouped[:].rearrange("p (t m j) -> p m t j", t=PACK, j=PACK)[:, m0 : m0 + 32],
+                    w1_raw[a, b][:].rearrange("p j (m t) -> p m t j", t=PACK)[:, m0 : m0 + 32],
+                )
             codes = held([P, KP], U32, "w1_q%d%d" % (a, b))
             scales = held([P, KP], U8, "w1_sc%d%d" % (a, b))
             nc.vector.quantize_mx(codes[:].bitcast(FP8X4), scales[:], grouped[:])
@@ -117,7 +116,9 @@ def tile_list_banquet_neighbour_scores_kernel(
 
         nc.vector.tensor_copy(v_sc[:], tab_sc[:].indirect(idx[:]))
         for q in range(4):
-            nc.gpsimd.dma_start(v_sc1[32 * q : 32 * q + 4, :].bitcast(I32), v_sc[32 * q + 4 : 32 * q + 8, :].bitcast(I32))
+            nc.sync.dma_start(v_sc1[32 * q : 32 * q + 4, :].bitcast(I32), v_sc[32 * q + 4 : 32 * q + 8, :].bitcast(I32))
+        tab.append(held([P, T], I32, "tab1"))
+        nc.sync.dma_start(tab[1][:], words(tab_words, 1))
         gather_v(0, 0)
         quantise_w1(0, 0)
         gather_v(0, 1)
@@ -143,7 +144,7 @@ def tile_list_banquet_neighbour_scores_kernel(
                 h_q[b, half] = held([P, BANK], U32, "h_q%d%d" % (b, half))
                 h_sc[b, half] = held([P, BANK], U8, "h_sc%d%d" % (b, half))
 
-        def stage1(u):
+        def unit(u):
             b, jq = divmod(u, S // UNIT)
             half, c0 = divmod(jq * UNIT, BANK)
             j0 = jq * UNIT
@@ -177,10 +178,12 @@ def tile_list_banquet_neighbour_scores_kernel(
                         stop=(a == 1 and t == PACK - 1),
                     )
 
-            for one_pass in (first_pass, second_pass):
-                for i in range(2):
-                    for a in range(2):
-                        one_pass(i, a)
+            def finish_unit():
+                epilogue(u, b, half, c0, first, second)
+
+            return first_pass, second_pass, finish_unit
+
+        def epilogue(u, b, half, c0, first, second):
             sq = ring.tile([P, 2, UNIT, 2], F32, name="sq", align_bytes=64)
             for pair in range(2):
                 nc.scalar.activation(sq[:, pair], first[pair][:].rearrange("p (s j) -> p j s", s=2), ACT.Square)
@@ -199,6 +202,14 @@ def tile_list_banquet_neighbour_scores_kernel(
                     h_q[b, half][:, cols].bitcast(FP8X4), h_sc[b, half][:, cols], h_bf[:, PACK * c : PACK * (c + step)]
                 )
 
+        def stage1(u):
+            first_pass, second_pass, finish_unit = unit(u)
+            for one_pass in (first_pass, second_pass):
+                for i in range(2):
+                    for a in range(2):
+                        one_pass(i, a)
+            finish_unit()
+
         v2 = []
 
         def gather_v2(b):
@@ -206,19 +217,35 @@ def tile_list_banquet_neighbour_scores_kernel(
             nc.vector.tensor_copy(t[:], tab2[:, b * T3 : (b + 1) * T3].bitcast(U32).indirect(idx2[:]))
             v2.append(t)
 
-        stage1(0)
+        opening = [unit(0), unit(1)]
+        for one_pass in range(2):
+            for passes in opening:
+                for i in range(2):
+                    passes[one_pass](i, 0)
+        for passes in opening:
+            for one_pass in range(2):
+                for i in range(2):
+                    passes[one_pass](i, 1)
         gather_v(1, 1)
         tab2 = held([P, 2 * T3], I32, "tab1")
         for b in range(2):
             nc.sync.dma_start(tab2[:, b * T3 : (b + 1) * T3], words(tab2_words, b))
-        stage1(1)
+        opening[0][2]()
+        opening[1][2]()
+        stage1(2)
+        stage1(3)
         quantise_w1(0, 1)
         allow_sb = ring.tile([P, S2 // P, NP], F32, name="w1_raw", align_bytes=64)
         nc.sync.dma_start(allow_sb[:], allow.rearrange("(m p) n -> p m n", p=P))
-        stage1(2)
         quantise_w1(1, 1)
-        stage1(3)
-        stage1(4)
+        first_pass, second_pass, finish_unit = unit(4)
+        for i in range(2):
+            for a in range(2):
+                second_pass(i, a)
+        for a in range(2):
+            for i in range(2):
+                first_pass(i, a)
+        finish_unit()
         gather_v2(0)
         stage1(5)
         gather_v2(1)
@@ -236,7 +263,7 @@ def tile_list_banquet_neighbour_scores_kernel(
                 nc.tensor.matmul_mx(
                     acc[:, lo:hi],
                     lhsT=v2[b][:, m * P : (m + 1) * P].bitcast(FP8X4),
-                    lhsT_scale=v2_sc[4 * b : P, m * P : (m + 1) * P],
+                    lhsT_scale=v2_sc[8 + 4 * b : P, m * P : (m + 1) * P],
                     rhs=h_q[b, half][:, lo:hi].bitcast(FP8X4),
                     rhs_scale=h_sc[b, half][:, lo:hi],
                     start=(i == 0),

@@ -51,7 +51,7 @@ def tile_list_banquet_neighbour_scores_kernel(
                 queue.dma_start(tile[32 * q + row : 32 * q + row + 8, :].bitcast(I32), src[:, 4 * q : 4 * q + 4, :].bitcast(I32))
 
         def load_w1(a, b):
-            t = ring.tile([P, PACK, KP], F32, name="w1_raw", align_bytes=64)
+            t = ring.tile([P, PACK, KP], F32, name="w1_raw", bufs=3, align_bytes=64)
             nc.sync.dma_start(t[:], w1[a * KP : (a + 1) * KP, b * KP : (b + 1) * KP].rearrange("(p j) c -> p j c", j=PACK))
             return t
 
@@ -64,15 +64,13 @@ def tile_list_banquet_neighbour_scores_kernel(
         nc.gpsimd.memset(tab2_sc[:].bitcast(I32), 0)
         nc.vector.memset(v_sc1[:].bitcast(I32), 0)
         load_packed_scales(nc.gpsimd, tab2_sc, tab2_scales, 8)
-        warm_in = held([P, 16], F32, "warm_in")
-        warm_out = held([P, 16], F32, "warm_out")
-        nc.vector.memset(warm_in[:], 0.0)
-        nc.scalar.activation(warm_out[:], warm_in[:], ACT.Exp)
 
         tab = [held([P, T], I32, "tab0")]
         nc.sync.dma_start(tab[0][:, : T // 2], words(tab_words, 0)[:, : T // 2])
         idx = load_list(offs, "idx")
-        load_packed_scales(nc.sync, tab_sc, tab_scales, 0)
+        nc.sync.dma_start(tab_sc[4:P:8, :].bitcast(I32), tab_scales[1].bitcast(I32))
+        for q in range(4):
+            nc.sync.dma_start(tab_sc[32 * q : 32 * q + 4, :].bitcast(I32), tab_scales[0, 4 * q : 4 * q + 4, :].bitcast(I32))
         nc.sync.dma_start(tab[0][:, T // 2 :], words(tab_words, 0)[:, T // 2 :])
         w1_raw = {(0, 0): load_w1(0, 0)}
         w4_raw = held([P, 2, 2 * H], U8, "w4_raw")
@@ -82,8 +80,9 @@ def tile_list_banquet_neighbour_scores_kernel(
                 w4_sc_raw[32 * q : 32 * q + 4].bitcast(I32),
                 w4_scales[:, 4 * q : 4 * q + 4, :].rearrange("a r c -> r a c").bitcast(I32),
             )
-        w1_raw[1, 0] = load_w1(1, 0)
         idx2 = load_list(offs2, "idx2")
+        tab.append(held([P, T], I32, "tab1"))
+        nc.sync.dma_start(tab[1][:], words(tab_words, 1))
 
         v_sc = held([P, S], U8, "v_sc")
         v = {}
@@ -94,13 +93,14 @@ def tile_list_banquet_neighbour_scores_kernel(
             nc.vector.tensor_copy(t[:], tab[a][:].bitcast(U32).indirect(idx[:, 32 * half : 32 * (half + 1)]))
             v[a, half] = t
 
-        def quantise_w1(a, b):
+        def quantise_w1(a, b, on_vector=0):
             grouped = ring.tile([P, PACK * KP], BF16, name="w1_bf", align_bytes=64)
-            for m0 in range(0, P, 32):
-                nc.scalar.copy(
-                    grouped[:].rearrange("p (t m j) -> p m t j", t=PACK, j=PACK)[:, m0 : m0 + 32],
-                    w1_raw[a, b][:].rearrange("p j (m t) -> p m t j", t=PACK)[:, m0 : m0 + 32],
-                )
+            dst = grouped[:].rearrange("p (t m j) -> p m t j", t=PACK, j=PACK)
+            src = w1_raw[a, b][:].rearrange("p j (m t) -> p m t j", t=PACK)
+            for m0 in range(0, P - on_vector, 32):
+                nc.scalar.copy(dst[:, m0 : m0 + 32], src[:, m0 : m0 + 32])
+            if on_vector:
+                nc.vector.tensor_copy(dst[:, P - on_vector :], src[:, P - on_vector :])
             codes = held([P, KP], U32, "w1_q%d%d" % (a, b))
             scales = held([P, KP], U8, "w1_sc%d%d" % (a, b))
             nc.vector.quantize_mx(codes[:].bitcast(FP8X4), scales[:], grouped[:])
@@ -116,27 +116,30 @@ def tile_list_banquet_neighbour_scores_kernel(
 
         nc.vector.tensor_copy(v_sc[:], tab_sc[:].indirect(idx[:]))
         for q in range(4):
-            nc.sync.dma_start(v_sc1[32 * q : 32 * q + 4, :].bitcast(I32), v_sc[32 * q + 4 : 32 * q + 8, :].bitcast(I32))
-        tab.append(held([P, T], I32, "tab1"))
-        nc.sync.dma_start(tab[1][:], words(tab_words, 1))
-        gather_v(0, 0)
-        quantise_w1(0, 0)
-        gather_v(0, 1)
+            nc.sync.dma_start(v_sc1[32 * q : 32 * q + 4, :].bitcast(I32), v_sc[32 * q + 4 : 32 * q + 32 : 8, :].bitcast(I32))
+        w1_raw[1, 0] = load_w1(1, 0)
         w1_raw[0, 1] = load_w1(0, 1)
+        gather_v(0, 0)
+        gather_v(0, 1)
+        quantise_w1(0, 0)
+        w1_raw[1, 1] = load_w1(1, 1)
+        p1 = load_list(pos1, "p1")
+        p2 = load_list(pos2, "p2")
         w4_sc = held([P, 2 * H], U8, "w4_sc")
         nc.vector.tensor_copy(
             w4_sc[:].rearrange("p (g t m) -> p g t m", t=PACK, m=P),
             w4_sc_raw[:].rearrange("p a (b m t) -> p (a b) t m", t=PACK, m=P),
         )
         deal_w4(0)
-        quantise_w1(1, 0)
-        w1_raw[1, 1] = load_w1(1, 1)
-        p1 = load_list(pos1, "p1")
-        p2 = load_list(pos2, "p2")
         deal_w4(1)
         v2_sc = held([P, S2], U8, "v2_sc")
         nc.vector.tensor_copy(v2_sc[:], tab2_sc[:].indirect(idx2[:]))
         gather_v(1, 0)
+        gather_v(1, 1)
+        tab2 = held([P, 2 * T3], I32, "tab1")
+        for b in range(2):
+            nc.sync.dma_start(tab2[:, b * T3 : (b + 1) * T3], words(tab2_words, b))
+        quantise_w1(1, 0, on_vector=96)
 
         h_q, h_sc = {}, {}
         for b in range(2):
@@ -160,7 +163,7 @@ def tile_list_banquet_neighbour_scores_kernel(
                         lhsT=w1_q[a, b][:, t * P : (t + 1) * P].bitcast(FP8X4),
                         lhsT_scale=w1_sc[a, b][:, t * P : (t + 1) * P],
                         rhs=v[a, half][:, c0 : c0 + UNIT].bitcast(FP8X4),
-                        rhs_scale=v_sc[4 * a : P, j0 : j0 + UNIT],
+                        rhs_scale=(v_sc, v_sc1)[a][:, j0 : j0 + UNIT],
                         start=(a == 0 and s == 0),
                         stop=(a == 1 and s == 1),
                     )
@@ -218,24 +221,18 @@ def tile_list_banquet_neighbour_scores_kernel(
             v2.append(t)
 
         opening = [unit(0), unit(1)]
-        for one_pass in range(2):
+        for one_pass, a in ((0, 0), (1, 0), (1, 1)):
             for passes in opening:
                 for i in range(2):
-                    passes[one_pass](i, 0)
+                    passes[one_pass](i, a)
         for passes in opening:
-            for one_pass in range(2):
-                for i in range(2):
-                    passes[one_pass](i, 1)
-        gather_v(1, 1)
-        tab2 = held([P, 2 * T3], I32, "tab1")
-        for b in range(2):
-            nc.sync.dma_start(tab2[:, b * T3 : (b + 1) * T3], words(tab2_words, b))
-        opening[0][2]()
-        opening[1][2]()
+            for i in range(2):
+                passes[0](i, 1)
+            passes[2]()
         stage1(2)
         stage1(3)
         quantise_w1(0, 1)
-        allow_sb = ring.tile([P, S2 // P, NP], F32, name="w1_raw", align_bytes=64)
+        allow_sb = ring.tile([P, S2 // P, NP], F32, name="w1_raw", bufs=3, align_bytes=64)
         nc.sync.dma_start(allow_sb[:], allow.rearrange("(m p) n -> p m n", p=P))
         quantise_w1(1, 1)
         first_pass, second_pass, finish_unit = unit(4)
@@ -254,26 +251,28 @@ def tile_list_banquet_neighbour_scores_kernel(
 
         e = [held([P, S], F32, "e%d" % m) for m in range(S2 // P)]
 
-        def scores(m, half):
-            acc = bank(4 * half + m)
-            pieces = [(0, 0, BANK), (1, 0, BANK)]
-            if half == 1:
-                pieces = [(0, 0, BANK), (1, 0, UNIT), (1, UNIT, UNIT + P), (1, UNIT + P, BANK)]
-            for i, (b, lo, hi) in enumerate(pieces):
+        def scores(m, where, half, lo, hi, pieces):
+            acc = bank(where)
+            for i, (b, c0, c1) in enumerate(pieces):
                 nc.tensor.matmul_mx(
-                    acc[:, lo:hi],
+                    acc[:, c0:c1],
                     lhsT=v2[b][:, m * P : (m + 1) * P].bitcast(FP8X4),
                     lhsT_scale=v2_sc[8 + 4 * b : P, m * P : (m + 1) * P],
-                    rhs=h_q[b, half][:, lo:hi].bitcast(FP8X4),
-                    rhs_scale=h_sc[b, half][:, lo:hi],
+                    rhs=h_q[b, half][:, c0:c1].bitcast(FP8X4),
+                    rhs_scale=h_sc[b, half][:, c0:c1],
                     start=(i == 0),
                     stop=(i == len(pieces) - 1),
                 )
-            nc.scalar.copy(e[m][:, half * BANK : (half + 1) * BANK], acc[:])
+            nc.scalar.copy(e[m][:, half * BANK + lo : half * BANK + hi], acc[:, lo:hi])
 
-        for m in range(S2 // P):
-            for half in range(2):
-                scores(m, half)
+        whole = [(0, 0, BANK), (1, 0, BANK)]
+        cut = UNIT + P
+        scores(0, 0, 0, 0, BANK, whole)
+        scores(0, 4, 1, 0, cut, [(b, c0, c1) for b in range(2) for c0, c1 in ((0, UNIT), (UNIT, cut))])
+        scores(0, 5, 1, cut, BANK, [(b, cut, BANK) for b in range(2)])
+        for m in range(1, S2 // P):
+            scores(m, m, 0, 0, BANK, whole)
+            scores(m, (5 + m) % 8, 1, 0, BANK, whole)
 
         guest, agree = {}, {}
 

@@ -69,16 +69,15 @@ def tile_list_banquet_neighbour_scores_kernel(
         nc.sync.dma_start(tab[0][:, : T // 2], words(tab_words, 0)[:, : T // 2])
         idx = load_list(offs, "idx")
         nc.sync.dma_start(tab_sc[4:P:8, :].bitcast(I32), tab_scales[1].bitcast(I32))
-        for q in range(4):
-            nc.sync.dma_start(tab_sc[32 * q : 32 * q + 4, :].bitcast(I32), tab_scales[0, 4 * q : 4 * q + 4, :].bitcast(I32))
+        for r in range(4):
+            nc.sync.dma_start(tab_sc[r:P:32, :].bitcast(I32), tab_scales[0, r:16:4, :].bitcast(I32))
         nc.sync.dma_start(tab[0][:, T // 2 :], words(tab_words, 0)[:, T // 2 :])
         w1_raw = {(0, 0): load_w1(0, 0)}
         w4_raw = held([P, 2, 2 * H], U8, "w4_raw")
         nc.sync.dma_start(w4_raw[:].bitcast(I32), w4_words.rearrange("a p c -> p a c").bitcast(I32))
-        for q in range(4):
+        for r in range(4):
             nc.sync.dma_start(
-                w4_sc_raw[32 * q : 32 * q + 4].bitcast(I32),
-                w4_scales[:, 4 * q : 4 * q + 4, :].rearrange("a r c -> r a c").bitcast(I32),
+                w4_sc_raw[r:P:32].bitcast(I32), w4_scales[:, r:16:4, :].rearrange("a q c -> q a c").bitcast(I32)
             )
         idx2 = load_list(offs2, "idx2")
         tab.append(held([P, T], I32, "tab1"))
@@ -115,8 +114,8 @@ def tile_list_banquet_neighbour_scores_kernel(
             w4_q[b] = t
 
         nc.vector.tensor_copy(v_sc[:], tab_sc[:].indirect(idx[:]))
-        for q in range(4):
-            nc.sync.dma_start(v_sc1[32 * q : 32 * q + 4, :].bitcast(I32), v_sc[32 * q + 4 : 32 * q + 32 : 8, :].bitcast(I32))
+        for r in range(4):
+            nc.sync.dma_start(v_sc1[r:P:32, :].bitcast(I32), v_sc[8 * r + 4 : P : 32, :].bitcast(I32))
         w1_raw[1, 0] = load_w1(1, 0)
         w1_raw[0, 1] = load_w1(0, 1)
         gather_v(0, 0)
@@ -141,11 +140,23 @@ def tile_list_banquet_neighbour_scores_kernel(
             nc.sync.dma_start(tab2[:, b * T3 : (b + 1) * T3], words(tab2_words, b))
         quantise_w1(1, 0, on_vector=96)
 
-        h_q, h_sc = {}, {}
+        h_q, h_sc, h_bf = {}, {}, {}
         for b in range(2):
             for half in range(2):
-                h_q[b, half] = held([P, BANK], U32, "h_q%d%d" % (b, half))
                 h_sc[b, half] = held([P, BANK], U8, "h_sc%d%d" % (b, half))
+        for u in (0, 2, 4):
+            both = held([P, 2 * UNIT * PACK], BF16, "h_bf%d" % u)
+            h_bf[u, u + 1] = both[:]
+            h_bf[u] = both[:, : UNIT * PACK]
+            h_bf[u + 1] = both[:, UNIT * PACK :]
+        for u in (6, 7):
+            single = held([P, UNIT * PACK], BF16, "h_bf%d" % u)
+            h_bf[u] = single[:]
+        for half in range(2):
+            h_q[1, half] = held([P, BANK], U32, "h_q1%d" % half)
+
+        def quantise_h(b, half, lo, hi, src):
+            nc.vector.quantize_mx(h_q[b, half][:, lo:hi].bitcast(FP8X4), h_sc[b, half][:, lo:hi], src)
 
         def unit(u):
             b, jq = divmod(u, S // UNIT)
@@ -190,19 +201,12 @@ def tile_list_banquet_neighbour_scores_kernel(
             sq = ring.tile([P, 2, UNIT, 2], F32, name="sq", align_bytes=64)
             for pair in range(2):
                 nc.scalar.activation(sq[:, pair], first[pair][:].rearrange("p (s j) -> p j s", s=2), ACT.Square)
-            h_bf = ring.tile([P, UNIT * PACK], BF16, name="h_bf", align_bytes=64)
             for g in range(2):
                 nc.vector.tensor_tensor(
-                    h_bf[:, g * BANK : (g + 1) * BANK].rearrange("p (j r s) -> p j r s", r=2, s=2),
+                    h_bf[u][:, g * BANK : (g + 1) * BANK].rearrange("p (j r s) -> p j r s", r=2, s=2),
                     second[g][:].rearrange("p (r s j) -> p j r s", r=2, s=2),
                     sq[:, :, g * P : (g + 1) * P, :].rearrange("p r j s -> p j r s"),
                     ALU.subtract,
-                )
-            step = P if u == 7 else UNIT
-            for c in range(0, UNIT, step):
-                cols = slice(c0 + c, c0 + c + step)
-                nc.vector.quantize_mx(
-                    h_q[b, half][:, cols].bitcast(FP8X4), h_sc[b, half][:, cols], h_bf[:, PACK * c : PACK * (c + step)]
                 )
 
         def stage1(u):
@@ -213,12 +217,15 @@ def tile_list_banquet_neighbour_scores_kernel(
                         one_pass(i, a)
             finish_unit()
 
-        v2 = []
+        v2 = {}
 
-        def gather_v2(b):
-            t = held([P, S2], U32, "v2_%d" % b)
-            nc.vector.tensor_copy(t[:], tab2[:, b * T3 : (b + 1) * T3].bitcast(U32).indirect(idx2[:]))
-            v2.append(t)
+        def gather_v2(part, name):
+            t = held([P, 2, S2 // 2], U32, name)
+            for b in range(2):
+                nc.vector.tensor_copy(
+                    t[:, b, :], tab2[:, b * T3 : (b + 1) * T3].bitcast(U32).indirect(idx2[:, 16 * part : 16 * (part + 1)])
+                )
+            v2[part] = t
 
         opening = [unit(0), unit(1)]
         for one_pass, a in ((0, 0), (1, 0), (1, 1)):
@@ -231,10 +238,12 @@ def tile_list_banquet_neighbour_scores_kernel(
             passes[2]()
         stage1(2)
         stage1(3)
-        quantise_w1(0, 1)
+        quantise_w1(0, 1, on_vector=64)
         allow_sb = ring.tile([P, S2 // P, NP], F32, name="w1_raw", bufs=3, align_bytes=64)
         nc.sync.dma_start(allow_sb[:], allow.rearrange("(m p) n -> p m n", p=P))
-        quantise_w1(1, 1)
+        quantise_w1(1, 1, on_vector=64)
+        for half in range(2):
+            h_q[0, half] = ring.tile([P, BANK], U32, name="w1_bf", align_bytes=64)
         first_pass, second_pass, finish_unit = unit(4)
         for i in range(2):
             for a in range(2):
@@ -243,11 +252,17 @@ def tile_list_banquet_neighbour_scores_kernel(
             for i in range(2):
                 first_pass(i, a)
         finish_unit()
-        gather_v2(0)
+        quantise_h(0, 0, 0, BANK, h_bf[0, 1])
         stage1(5)
-        gather_v2(1)
+        quantise_h(0, 1, 0, BANK, h_bf[2, 3])
+        gather_v2(0, "v2_early")
         stage1(6)
+        quantise_h(1, 0, 0, BANK, h_bf[4, 5])
+        quantise_h(1, 1, 0, UNIT, h_bf[6])
         stage1(7)
+        for g in range(2):
+            quantise_h(1, 1, UNIT + g * P, UNIT + (g + 1) * P, h_bf[7][:, g * BANK : (g + 1) * BANK])
+        gather_v2(1, "h_bf7")
 
         e = [held([P, S], F32, "e%d" % m) for m in range(S2 // P)]
 
@@ -256,7 +271,7 @@ def tile_list_banquet_neighbour_scores_kernel(
             for i, (b, c0, c1) in enumerate(pieces):
                 nc.tensor.matmul_mx(
                     acc[:, c0:c1],
-                    lhsT=v2[b][:, m * P : (m + 1) * P].bitcast(FP8X4),
+                    lhsT=v2[m // 2][:, b, (m % 2) * P : (m % 2 + 1) * P].bitcast(FP8X4),
                     lhsT_scale=v2_sc[8 + 4 * b : P, m * P : (m + 1) * P],
                     rhs=h_q[b, half][:, c0:c1].bitcast(FP8X4),
                     rhs_scale=h_sc[b, half][:, c0:c1],

@@ -2,7 +2,7 @@ from contextlib import ExitStack
 
 import concourse.mybir as mybir
 
-K, H, T, S, S2, T3, NP = 1024, 1024, 4096, 1024, 512, 2048, 512
+K, H, T, S, S2, T3, PAIRS = 1024, 1024, 4096, 1024, 512, 2048, 512
 FLOPS = 2 * (2 * K * H * S + H * S2 * S)
 
 F32 = mybir.dt.float32
@@ -21,6 +21,11 @@ PACK = 4
 KP = P * PACK
 BANK = 512
 UNIT = 256
+PER_COL = 16
+QUAD = 32
+THEME_ROW = 8
+PIECE = 32
+VECTOR_SHARE = {(0, 0): 0, (1, 0): 96, (0, 1): 32, (1, 1): 64}
 
 
 def tile_list_banquet_neighbour_scores_kernel(
@@ -38,90 +43,107 @@ def tile_list_banquet_neighbour_scores_kernel(
         def bank(i):
             return psum.tile([P, BANK], F32, name="bank%d" % i)
 
+        def staging():
+            return ring.tile([P, PACK, KP], F32, name="staging", bufs=3, align_bytes=64)
+
         def load_list(src, name):
-            t = keep.tile([P, src.shape[1]], U16, name=name)
-            nc.sync.dma_start(t[:], src)
-            return t
+            tile = keep.tile([P, src.shape[1]], U16, name=name)
+            nc.sync.dma_start(tile[:], src)
+            return tile
 
         def words(src, a):
             return src[a].rearrange("p t i -> p (t i)").bitcast(I32)
 
-        def load_packed_scales(queue, tile, src, row):
-            for q in range(4):
-                queue.dma_start(tile[32 * q + row : 32 * q + row + 8, :].bitcast(I32), src[:, 4 * q : 4 * q + 4, :].bitcast(I32))
-
         def load_w1(a, b):
-            t = ring.tile([P, PACK, KP], F32, name="w1_raw", bufs=3, align_bytes=64)
-            nc.sync.dma_start(t[:], w1[a * KP : (a + 1) * KP, b * KP : (b + 1) * KP].rearrange("(p j) c -> p j c", j=PACK))
-            return t
+            tile = staging()
+            nc.sync.dma_start(tile[:], w1[a * KP : (a + 1) * KP, b * KP : (b + 1) * KP].rearrange("(p j) c -> p j c", j=PACK))
+            return tile
+
+        def load_w4(b):
+            tile = held([P, 2, 2 * KP], U8, "w4_raw%d" % b)
+            nc.sync.dma_start(
+                tile[:].bitcast(I32), w4_words[:, :, 2 * KP * b : 2 * KP * (b + 1)].rearrange("a p c -> p a c").bitcast(I32)
+            )
+            return tile
 
         tab_sc = held([P, T], U8, "tab_sc")
         w4_sc_raw = held([P, 2, H], U8, "w4_sc_raw")
-        v_sc1 = held([P, S], U8, "v_sc1")
+        v_sc = [held([P, S], U8, "v_sc%d" % a) for a in range(2)]
+        tab2_sc = held([P, T3], U8, "tab2_sc")
         nc.vector.memset(tab_sc[:].bitcast(I32), 0)
         nc.vector.memset(w4_sc_raw[:].bitcast(I32), 0)
-        tab2_sc = held([P, T3], U8, "tab2_sc")
         nc.gpsimd.memset(tab2_sc[:].bitcast(I32), 0)
-        nc.vector.memset(v_sc1[:].bitcast(I32), 0)
-        load_packed_scales(nc.gpsimd, tab2_sc, tab2_scales, 8)
+        for a in range(2):
+            nc.vector.memset(v_sc[a][:].bitcast(I32), 0)
+
+        for q in range(4):
+            rows = slice(QUAD * q + THEME_ROW, QUAD * q + THEME_ROW + 8)
+            nc.gpsimd.dma_start(tab2_sc[rows, :].bitcast(I32), tab2_scales[:, 4 * q : 4 * q + 4, :].bitcast(I32))
 
         tab = [held([P, T], I32, "tab0")]
         nc.sync.dma_start(tab[0][:, : T // 2], words(tab_words, 0)[:, : T // 2])
         idx = load_list(offs, "idx")
-        nc.sync.dma_start(tab_sc[4:P:8, :].bitcast(I32), tab_scales[1].bitcast(I32))
-        for r in range(4):
-            nc.sync.dma_start(tab_sc[r:P:32, :].bitcast(I32), tab_scales[0, r:16:4, :].bitcast(I32))
+        nc.sync.dma_start(tab_sc[0:P:4, :].bitcast(I32), tab_scales.rearrange("a q t -> (a q) t").bitcast(I32))
         nc.sync.dma_start(tab[0][:, T // 2 :], words(tab_words, 0)[:, T // 2 :])
         w1_raw = {(0, 0): load_w1(0, 0)}
-        w4_raw = held([P, 2, 2 * H], U8, "w4_raw")
-        nc.sync.dma_start(w4_raw[:].bitcast(I32), w4_words.rearrange("a p c -> p a c").bitcast(I32))
+        w4_raw = [load_w4(0)]
         for r in range(4):
             nc.sync.dma_start(
-                w4_sc_raw[r:P:32].bitcast(I32), w4_scales[:, r:16:4, :].rearrange("a q c -> q a c").bitcast(I32)
+                w4_sc_raw[r:P:QUAD].bitcast(I32), w4_scales[:, r:16:4, :].rearrange("a q c -> q a c").bitcast(I32)
             )
         idx2 = load_list(offs2, "idx2")
         tab.append(held([P, T], I32, "tab1"))
-        nc.sync.dma_start(tab[1][:], words(tab_words, 1))
+        nc.sync.dma_start(tab[1][:, : T // 2], words(tab_words, 1)[:, : T // 2])
 
-        v_sc = held([P, S], U8, "v_sc")
-        v = {}
-        w1_q, w1_sc, w4_q = {}, {}, {}
+        v_sc_rows = held([P, S], U8, "v_sc_rows")
+        v, w1_q, w1_sc, w4_q = {}, {}, {}, {}
+
+        def place_v_scales(a):
+            for r in range(4):
+                nc.sync.dma_start(v_sc[a][r:P:QUAD, :].bitcast(I32), v_sc_rows[64 * a + 4 * r : 64 * (a + 1) : 16, :].bitcast(I32))
 
         def gather_v(a, half):
-            t = held([P, BANK], U32, "v%d%d" % (a, half))
-            nc.vector.tensor_copy(t[:], tab[a][:].bitcast(U32).indirect(idx[:, 32 * half : 32 * (half + 1)]))
-            v[a, half] = t
+            cols = slice(half * BANK // PER_COL, (half + 1) * BANK // PER_COL)
+            v[a, half] = held([P, BANK], U32, "v%d%d" % (a, half))
+            nc.vector.tensor_copy(v[a, half][:], tab[a][:].bitcast(U32).indirect(idx[:, cols]))
 
-        def quantise_w1(a, b, on_vector=0):
+        def quantise_w1(a, b, calls):
             grouped = ring.tile([P, PACK * KP], BF16, name="w1_bf", align_bytes=64)
             dst = grouped[:].rearrange("p (t m j) -> p m t j", t=PACK, j=PACK)
             src = w1_raw[a, b][:].rearrange("p j (m t) -> p m t j", t=PACK)
-            for m0 in range(0, P - on_vector, 32):
-                nc.scalar.copy(dst[:, m0 : m0 + 32], src[:, m0 : m0 + 32])
-            if on_vector:
-                nc.vector.tensor_copy(dst[:, P - on_vector :], src[:, P - on_vector :])
-            codes = held([P, KP], U32, "w1_q%d%d" % (a, b))
-            scales = held([P, KP], U8, "w1_sc%d%d" % (a, b))
-            nc.vector.quantize_mx(codes[:].bitcast(FP8X4), scales[:], grouped[:])
-            w1_q[a, b], w1_sc[a, b] = codes, scales
+            on_scalar = P - VECTOR_SHARE[a, b]
+            for m0 in range(0, on_scalar, PIECE):
+                nc.scalar.copy(dst[:, m0 : m0 + PIECE], src[:, m0 : m0 + PIECE])
+            if on_scalar < P:
+                nc.vector.tensor_copy(dst[:, on_scalar:], src[:, on_scalar:])
+            w1_q[a, b] = held([P, KP], U32, "w1_q%d%d" % (a, b))
+            w1_sc[a, b] = held([P, KP], U8, "w1_sc%d%d" % (a, b))
+            step = KP // calls
+            for c in range(0, KP, step):
+                nc.vector.quantize_mx(
+                    w1_q[a, b][:, c : c + step].bitcast(FP8X4),
+                    w1_sc[a, b][:, c : c + step],
+                    grouped[:, PACK * c : PACK * (c + step)],
+                )
 
         def deal_w4(b):
-            t = held([P, 2, 2 * KP], U8, "w4_q%d" % b)
+            w4_q[b] = held([P, 2, 2 * KP], U8, "w4_q%d" % b)
             nc.vector.tensor_copy(
-                t[:].bitcast(U16).rearrange("p a (t m) -> p a t m", t=PACK),
-                w4_raw[:, :, 2 * KP * b : 2 * KP * (b + 1)].bitcast(U16).rearrange("p a (m t) -> p a t m", t=PACK),
+                w4_q[b][:].bitcast(U16).rearrange("p a (t m) -> p a t m", t=PACK),
+                w4_raw[b][:].bitcast(U16).rearrange("p a (m t) -> p a t m", t=PACK),
             )
-            w4_q[b] = t
 
-        nc.vector.tensor_copy(v_sc[:], tab_sc[:].indirect(idx[:]))
-        for r in range(4):
-            nc.sync.dma_start(v_sc1[r:P:32, :].bitcast(I32), v_sc[8 * r + 4 : P : 32, :].bitcast(I32))
+        nc.vector.tensor_copy(v_sc_rows[:], tab_sc[:].indirect(idx[:]))
+        place_v_scales(0)
+        nc.sync.dma_start(tab[1][:, T // 2 :], words(tab_words, 1)[:, T // 2 :])
+        place_v_scales(1)
         w1_raw[1, 0] = load_w1(1, 0)
         w1_raw[0, 1] = load_w1(0, 1)
         gather_v(0, 0)
         gather_v(0, 1)
-        quantise_w1(0, 0)
+        quantise_w1(0, 0, calls=1)
         w1_raw[1, 1] = load_w1(1, 1)
+        w4_raw.append(load_w4(1))
         p1 = load_list(pos1, "p1")
         p2 = load_list(pos2, "p2")
         w4_sc = held([P, 2 * H], U8, "w4_sc")
@@ -130,7 +152,6 @@ def tile_list_banquet_neighbour_scores_kernel(
             w4_sc_raw[:].rearrange("p a (b m t) -> p (a b) t m", t=PACK, m=P),
         )
         deal_w4(0)
-        deal_w4(1)
         v2_sc = held([P, S2], U8, "v2_sc")
         nc.vector.tensor_copy(v2_sc[:], tab2_sc[:].indirect(idx2[:]))
         gather_v(1, 0)
@@ -138,17 +159,16 @@ def tile_list_banquet_neighbour_scores_kernel(
         tab2 = held([P, 2 * T3], I32, "tab1")
         for b in range(2):
             nc.sync.dma_start(tab2[:, b * T3 : (b + 1) * T3], words(tab2_words, b))
-        quantise_w1(1, 0, on_vector=96)
+        quantise_w1(1, 0, calls=2)
 
-        h_q, h_sc, h_bf = {}, {}, {}
+        h_q, h_sc, h_bf, h_two = {}, {}, {}, {}
         for b in range(2):
             for half in range(2):
                 h_sc[b, half] = held([P, BANK], U8, "h_sc%d%d" % (b, half))
         for u in (0, 2, 4):
-            both = held([P, 2 * UNIT * PACK], BF16, "h_bf%d" % u)
-            h_bf[u, u + 1] = both[:]
-            h_bf[u] = both[:, : UNIT * PACK]
-            h_bf[u + 1] = both[:, UNIT * PACK :]
+            h_two[u] = held([P, 2 * UNIT * PACK], BF16, "h_bf%d" % u)
+            h_bf[u] = h_two[u][:, : UNIT * PACK]
+            h_bf[u + 1] = h_two[u][:, UNIT * PACK :]
         for u in (6, 7):
             single = held([P, UNIT * PACK], BF16, "h_bf%d" % u)
             h_bf[u] = single[:]
@@ -158,108 +178,109 @@ def tile_list_banquet_neighbour_scores_kernel(
         def quantise_h(b, half, lo, hi, src):
             nc.vector.quantize_mx(h_q[b, half][:, lo:hi].bitcast(FP8X4), h_sc[b, half][:, lo:hi], src)
 
-        def unit(u):
-            b, jq = divmod(u, S // UNIT)
-            half, c0 = divmod(jq * UNIT, BANK)
-            j0 = jq * UNIT
+        squared, linear = {}, {}
+
+        def open_unit(u):
             base = 4 * (u % 2)
-            first = [bank(base), bank(base + 1)]
-            second = [bank(base + 2), bank(base + 3)]
+            squared[u] = [bank(base), bank(base + 1)]
+            linear[u] = [bank(base + 2), bank(base + 3)]
 
-            def first_pass(pair, a):
-                for s in range(2):
-                    t = 2 * pair + s
-                    nc.tensor.matmul_mx(
-                        first[pair][:, s * UNIT : (s + 1) * UNIT],
-                        lhsT=w1_q[a, b][:, t * P : (t + 1) * P].bitcast(FP8X4),
-                        lhsT_scale=w1_sc[a, b][:, t * P : (t + 1) * P],
-                        rhs=v[a, half][:, c0 : c0 + UNIT].bitcast(FP8X4),
-                        rhs_scale=(v_sc, v_sc1)[a][:, j0 : j0 + UNIT],
-                        start=(a == 0 and s == 0),
-                        stop=(a == 1 and s == 1),
-                    )
+        def guests(u):
+            b, quarter = divmod(u, S // UNIT)
+            half, c0 = divmod(quarter * UNIT, BANK)
+            return b, half, c0, quarter * UNIT
 
-            def second_pass(g, a):
-                for t in range(PACK):
-                    sc0 = (2 * a + b) * KP + t * P
-                    nc.tensor.matmul_mx(
-                        second[g][:, t * P : (t + 1) * P],
-                        lhsT=w4_q[b][:, a, 2 * t * P : 2 * (t + 1) * P].bitcast(FP4X4),
-                        lhsT_scale=w4_sc[:, sc0 : sc0 + P],
-                        rhs=v[a, half][:, c0 + g * P : c0 + (g + 1) * P].bitcast(FP8X4),
-                        rhs_scale=(v_sc, v_sc1)[a][:, j0 + g * P : j0 + (g + 1) * P],
-                        start=(a == 0 and t == 0),
-                        stop=(a == 1 and t == PACK - 1),
-                    )
+        def w1_pass(u, pair, a):
+            b, half, c0, j0 = guests(u)
+            for s in range(2):
+                t = 2 * pair + s
+                nc.tensor.matmul_mx(
+                    squared[u][pair][:, s * UNIT : (s + 1) * UNIT],
+                    lhsT=w1_q[a, b][:, t * P : (t + 1) * P].bitcast(FP8X4),
+                    lhsT_scale=w1_sc[a, b][:, t * P : (t + 1) * P],
+                    rhs=v[a, half][:, c0 : c0 + UNIT].bitcast(FP8X4),
+                    rhs_scale=v_sc[a][:, j0 : j0 + UNIT],
+                    start=(a == 0 and s == 0),
+                    stop=(a == 1 and s == 1),
+                )
 
-            def finish_unit():
-                epilogue(u, b, half, c0, first, second)
+        def w4_pass(u, g, a):
+            b, half, c0, j0 = guests(u)
+            for t in range(PACK):
+                sc0 = (2 * a + b) * KP + t * P
+                nc.tensor.matmul_mx(
+                    linear[u][g][:, t * P : (t + 1) * P],
+                    lhsT=w4_q[b][:, a, 2 * t * P : 2 * (t + 1) * P].bitcast(FP4X4),
+                    lhsT_scale=w4_sc[:, sc0 : sc0 + P],
+                    rhs=v[a, half][:, c0 + g * P : c0 + (g + 1) * P].bitcast(FP8X4),
+                    rhs_scale=v_sc[a][:, j0 + g * P : j0 + (g + 1) * P],
+                    start=(a == 0 and t == 0),
+                    stop=(a == 1 and t == PACK - 1),
+                )
 
-            return first_pass, second_pass, finish_unit
-
-        def epilogue(u, b, half, c0, first, second):
+        def close_unit(u):
             sq = ring.tile([P, 2, UNIT, 2], F32, name="sq", align_bytes=64)
             for pair in range(2):
-                nc.scalar.activation(sq[:, pair], first[pair][:].rearrange("p (s j) -> p j s", s=2), ACT.Square)
+                nc.scalar.activation(sq[:, pair], squared[u][pair][:].rearrange("p (s j) -> p j s", s=2), ACT.Square)
             for g in range(2):
                 nc.vector.tensor_tensor(
                     h_bf[u][:, g * BANK : (g + 1) * BANK].rearrange("p (j r s) -> p j r s", r=2, s=2),
-                    second[g][:].rearrange("p (r s j) -> p j r s", r=2, s=2),
+                    linear[u][g][:].rearrange("p (r s j) -> p j r s", r=2, s=2),
                     sq[:, :, g * P : (g + 1) * P, :].rearrange("p r j s -> p j r s"),
                     ALU.subtract,
                 )
 
-        def stage1(u):
-            first_pass, second_pass, finish_unit = unit(u)
-            for one_pass in (first_pass, second_pass):
+        def whole_unit(u):
+            open_unit(u)
+            for one_pass in (w1_pass, w4_pass):
                 for i in range(2):
                     for a in range(2):
-                        one_pass(i, a)
-            finish_unit()
+                        one_pass(u, i, a)
+            close_unit(u)
 
         v2 = {}
 
         def gather_v2(part, name):
-            t = held([P, 2, S2 // 2], U32, name)
+            cols = slice(part * S2 // 2 // PER_COL, (part + 1) * S2 // 2 // PER_COL)
+            v2[part] = held([P, 2, S2 // 2], U32, name)
             for b in range(2):
-                nc.vector.tensor_copy(
-                    t[:, b, :], tab2[:, b * T3 : (b + 1) * T3].bitcast(U32).indirect(idx2[:, 16 * part : 16 * (part + 1)])
-                )
-            v2[part] = t
+                nc.vector.tensor_copy(v2[part][:, b, :], tab2[:, b * T3 : (b + 1) * T3].bitcast(U32).indirect(idx2[:, cols]))
 
-        opening = [unit(0), unit(1)]
-        for one_pass, a in ((0, 0), (1, 0), (1, 1)):
-            for passes in opening:
+        for u in (0, 1):
+            open_unit(u)
+        for one_pass, a in ((w1_pass, 0), (w4_pass, 0), (w4_pass, 1)):
+            for u in (0, 1):
                 for i in range(2):
-                    passes[one_pass](i, a)
-        for passes in opening:
+                    one_pass(u, i, a)
+        for u in (0, 1):
             for i in range(2):
-                passes[0](i, 1)
-            passes[2]()
-        stage1(2)
-        stage1(3)
-        quantise_w1(0, 1, on_vector=64)
-        allow_sb = ring.tile([P, S2 // P, NP], F32, name="w1_raw", bufs=3, align_bytes=64)
+                w1_pass(u, i, 1)
+            close_unit(u)
+        whole_unit(2)
+        whole_unit(3)
+        deal_w4(1)
+        quantise_w1(0, 1, calls=1)
+        allow_sb = staging()
         nc.sync.dma_start(allow_sb[:], allow.rearrange("(m p) n -> p m n", p=P))
-        quantise_w1(1, 1, on_vector=64)
+        quantise_w1(1, 1, calls=1)
         for half in range(2):
             h_q[0, half] = ring.tile([P, BANK], U32, name="w1_bf", align_bytes=64)
-        first_pass, second_pass, finish_unit = unit(4)
+        open_unit(4)
         for i in range(2):
             for a in range(2):
-                second_pass(i, a)
+                w4_pass(4, i, a)
         for a in range(2):
             for i in range(2):
-                first_pass(i, a)
-        finish_unit()
-        quantise_h(0, 0, 0, BANK, h_bf[0, 1])
-        stage1(5)
-        quantise_h(0, 1, 0, BANK, h_bf[2, 3])
+                w1_pass(4, i, a)
+        close_unit(4)
+        quantise_h(0, 0, 0, BANK, h_two[0][:])
+        whole_unit(5)
+        quantise_h(0, 1, 0, BANK, h_two[2][:])
         gather_v2(0, "v2_early")
-        stage1(6)
-        quantise_h(1, 0, 0, BANK, h_bf[4, 5])
+        whole_unit(6)
+        quantise_h(1, 0, 0, BANK, h_two[4][:])
         quantise_h(1, 1, 0, UNIT, h_bf[6])
-        stage1(7)
+        whole_unit(7)
         for g in range(2):
             quantise_h(1, 1, UNIT + g * P, UNIT + (g + 1) * P, h_bf[7][:, g * BANK : (g + 1) * BANK])
         gather_v2(1, "h_bf7")
@@ -272,7 +293,7 @@ def tile_list_banquet_neighbour_scores_kernel(
                 nc.tensor.matmul_mx(
                     acc[:, c0:c1],
                     lhsT=v2[m // 2][:, b, (m % 2) * P : (m % 2 + 1) * P].bitcast(FP8X4),
-                    lhsT_scale=v2_sc[8 + 4 * b : P, m * P : (m + 1) * P],
+                    lhsT_scale=v2_sc[THEME_ROW + 4 * b : P, m * P : (m + 1) * P],
                     rhs=h_q[b, half][:, c0:c1].bitcast(FP8X4),
                     rhs_scale=h_sc[b, half][:, c0:c1],
                     start=(i == 0),
@@ -285,19 +306,23 @@ def tile_list_banquet_neighbour_scores_kernel(
         scores(0, 0, 0, 0, BANK, whole)
         scores(0, 4, 1, 0, cut, [(b, c0, c1) for b in range(2) for c0, c1 in ((0, UNIT), (UNIT, cut))])
         scores(0, 5, 1, cut, BANK, [(b, cut, BANK) for b in range(2)])
-        for m in range(1, S2 // P):
+        scores(1, 1, 0, 0, BANK, whole)
+        scores(1, 6, 1, 0, BANK, [(0, 0, BANK), (1, 0, UNIT), (1, UNIT, cut), (1, cut, BANK)])
+        for m, second_bank in ((2, 7), (3, 0)):
             scores(m, m, 0, 0, BANK, whole)
-            scores(m, (5 + m) % 8, 1, 0, BANK, whole)
+            scores(m, second_bank, 1, 0, BANK, whole)
 
         guest, agree = {}, {}
 
         def pick_guest(m):
-            guest[m] = held([P, NP], F32, "guest%d" % m)
+            guest[m] = held([P, PAIRS], F32, "guest%d" % m)
             nc.vector.tensor_copy(guest[m][:], e[m][:].indirect(p1[:]))
 
         def compare(m, lo, hi):
             gap = held([P, hi - lo], F32, "gap%d_%d" % (m, lo))
-            nc.vector.tensor_tensor(gap[:], e[m][:].indirect(p2[:, lo // 16 : hi // 16]), guest[m][:, lo:hi], ALU.subtract)
+            nc.vector.tensor_tensor(
+                gap[:], e[m][:].indirect(p2[:, lo // PER_COL : hi // PER_COL]), guest[m][:, lo:hi], ALU.subtract
+            )
             dist = held([P, hi - lo], F32, "dist%d_%d" % (m, lo))
             nc.scalar.activation(dist[:], gap[:], ACT.Abs)
             agree[m, lo] = held([P, hi - lo], F32, "agree%d_%d" % (m, lo))
@@ -310,15 +335,15 @@ def tile_list_banquet_neighbour_scores_kernel(
 
         pick_guest(0)
         pick_guest(1)
-        compare(0, 0, NP)
+        compare(0, 0, PAIRS)
         pick_guest(2)
-        compare(1, 0, NP)
-        finish(0, 0, NP)
+        compare(1, 0, PAIRS)
+        finish(0, 0, PAIRS)
         pick_guest(3)
-        compare(2, 0, NP)
-        finish(1, 0, NP)
-        compare(3, 0, NP // 2)
-        compare(3, NP // 2, NP)
-        finish(2, 0, NP)
-        finish(3, 0, NP // 2)
-        finish(3, NP // 2, NP)
+        compare(2, 0, PAIRS)
+        finish(1, 0, PAIRS)
+        compare(3, 0, PAIRS // 2)
+        compare(3, PAIRS // 2, PAIRS)
+        finish(2, 0, PAIRS)
+        finish(3, 0, PAIRS // 2)
+        finish(3, PAIRS // 2, PAIRS)

from contextlib import ExitStack

import concourse.mybir as mybir

K, H, T, S, S2, T3, PAIRS = 1024, 1024, 4096, 1024, 512, 2048, 512
FLOPS = 2 * (2 * K * H * S + H * S2 * S)

F32 = mybir.dt.float32
BF16 = mybir.dt.bfloat16
I32 = mybir.dt.int32
U32 = mybir.dt.uint32
U16 = mybir.dt.uint16
U8 = mybir.dt.uint8
FP8X4 = mybir.dt.float8_e4m3fn_x4
FP4X4 = mybir.dt.float4_e2m1fn_x4
ACT = mybir.ActivationFunctionType
ALU = mybir.AluOpType

P = 128
PACK = 4
KP = P * PACK
BANK = 512
UNIT = 256
PER_COL = 16
QUAD = 32
THEME_ROW = 8
PIECE = 32
VECTOR_SHARE = {(0, 0): 0, (1, 0): 96, (0, 1): 32, (1, 1): 64}


def tile_list_banquet_neighbour_scores_kernel(
    tc, tab_words, tab_scales, offs, w4_words, w4_scales, w1, tab2_words, tab2_scales, offs2, pos1, pos2, allow, out
):
    nc = tc.nc
    with ExitStack() as ctx:
        keep = ctx.enter_context(tc.tile_pool(name="keep", bufs=1))
        ring = ctx.enter_context(tc.tile_pool(name="ring", bufs=2))
        psum = ctx.enter_context(tc.psum_pool(name="psum", bufs=1))

        def held(shape, dtype, name):
            return keep.tile(shape, dtype, name=name, align_bytes=64)

        def bank(i):
            return psum.tile([P, BANK], F32, name="bank%d" % i)

        def staging():
            return ring.tile([P, PACK, KP], F32, name="staging", bufs=3, align_bytes=64)

        def load_list(src, name):
            tile = keep.tile([P, src.shape[1]], U16, name=name)
            nc.sync.dma_start(tile[:], src)
            return tile

        def words(src, a):
            return src[a].rearrange("p t i -> p (t i)").bitcast(I32)

        def load_w1(a, b):
            tile = staging()
            nc.sync.dma_start(tile[:], w1[a * KP : (a + 1) * KP, b * KP : (b + 1) * KP].rearrange("(p j) c -> p j c", j=PACK))
            return tile

        def load_w4(b):
            tile = held([P, 2, 2 * KP], U8, "w4_raw%d" % b)
            nc.sync.dma_start(
                tile[:].bitcast(I32), w4_words[:, :, 2 * KP * b : 2 * KP * (b + 1)].rearrange("a p c -> p a c").bitcast(I32)
            )
            return tile

        tab_sc = held([P, T], U8, "tab_sc")
        w4_sc_raw = held([P, 2, H], U8, "w4_sc_raw")
        v_sc = [held([P, S], U8, "v_sc%d" % a) for a in range(2)]
        tab2_sc = held([P, T3], U8, "tab2_sc")
        nc.vector.memset(tab_sc[:].bitcast(I32), 0)
        nc.vector.memset(w4_sc_raw[:].bitcast(I32), 0)
        nc.gpsimd.memset(tab2_sc[:].bitcast(I32), 0)
        for a in range(2):
            nc.vector.memset(v_sc[a][:].bitcast(I32), 0)

        for q in range(4):
            rows = slice(QUAD * q + THEME_ROW, QUAD * q + THEME_ROW + 8)
            nc.gpsimd.dma_start(tab2_sc[rows, :].bitcast(I32), tab2_scales[:, 4 * q : 4 * q + 4, :].bitcast(I32))

        tab = [held([P, T], I32, "tab0")]
        nc.sync.dma_start(tab[0][:, : T // 2], words(tab_words, 0)[:, : T // 2])
        idx = load_list(offs, "idx")
        nc.sync.dma_start(tab_sc[0:P:4, :].bitcast(I32), tab_scales.rearrange("a q t -> (a q) t").bitcast(I32))
        nc.sync.dma_start(tab[0][:, T // 2 :], words(tab_words, 0)[:, T // 2 :])
        w1_raw = {(0, 0): load_w1(0, 0)}
        w4_raw = [load_w4(0)]
        for r in range(4):
            nc.sync.dma_start(
                w4_sc_raw[r:P:QUAD].bitcast(I32), w4_scales[:, r:16:4, :].rearrange("a q c -> q a c").bitcast(I32)
            )
        idx2 = load_list(offs2, "idx2")
        tab.append(held([P, T], I32, "tab1"))
        nc.sync.dma_start(tab[1][:, : T // 2], words(tab_words, 1)[:, : T // 2])

        v_sc_rows = held([P, S], U8, "v_sc_rows")
        v, w1_q, w1_sc, w4_q = {}, {}, {}, {}

        def place_v_scales(a):
            for r in range(4):
                nc.sync.dma_start(v_sc[a][r:P:QUAD, :].bitcast(I32), v_sc_rows[64 * a + 4 * r : 64 * (a + 1) : 16, :].bitcast(I32))

        def gather_v(a, half):
            cols = slice(half * BANK // PER_COL, (half + 1) * BANK // PER_COL)
            v[a, half] = held([P, BANK], U32, "v%d%d" % (a, half))
            nc.vector.tensor_copy(v[a, half][:], tab[a][:].bitcast(U32).indirect(idx[:, cols]))

        def quantise_w1(a, b, calls):
            grouped = ring.tile([P, PACK * KP], BF16, name="w1_bf", align_bytes=64)
            dst = grouped[:].rearrange("p (t m j) -> p m t j", t=PACK, j=PACK)
            src = w1_raw[a, b][:].rearrange("p j (m t) -> p m t j", t=PACK)
            on_scalar = P - VECTOR_SHARE[a, b]
            for m0 in range(0, on_scalar, PIECE):
                nc.scalar.copy(dst[:, m0 : m0 + PIECE], src[:, m0 : m0 + PIECE])
            if on_scalar < P:
                nc.vector.tensor_copy(dst[:, on_scalar:], src[:, on_scalar:])
            w1_q[a, b] = held([P, KP], U32, "w1_q%d%d" % (a, b))
            w1_sc[a, b] = held([P, KP], U8, "w1_sc%d%d" % (a, b))
            step = KP // calls
            for c in range(0, KP, step):
                nc.vector.quantize_mx(
                    w1_q[a, b][:, c : c + step].bitcast(FP8X4),
                    w1_sc[a, b][:, c : c + step],
                    grouped[:, PACK * c : PACK * (c + step)],
                )

        def deal_w4(b):
            w4_q[b] = held([P, 2, 2 * KP], U8, "w4_q%d" % b)
            nc.vector.tensor_copy(
                w4_q[b][:].bitcast(U16).rearrange("p a (t m) -> p a t m", t=PACK),
                w4_raw[b][:].bitcast(U16).rearrange("p a (m t) -> p a t m", t=PACK),
            )

        nc.vector.tensor_copy(v_sc_rows[:], tab_sc[:].indirect(idx[:]))
        place_v_scales(0)
        nc.sync.dma_start(tab[1][:, T // 2 :], words(tab_words, 1)[:, T // 2 :])
        place_v_scales(1)
        w1_raw[1, 0] = load_w1(1, 0)
        w1_raw[0, 1] = load_w1(0, 1)
        gather_v(0, 0)
        gather_v(0, 1)
        quantise_w1(0, 0, calls=1)
        w1_raw[1, 1] = load_w1(1, 1)
        w4_raw.append(load_w4(1))
        p1 = load_list(pos1, "p1")
        p2 = load_list(pos2, "p2")
        w4_sc = held([P, 2 * H], U8, "w4_sc")
        nc.vector.tensor_copy(
            w4_sc[:].rearrange("p (g t m) -> p g t m", t=PACK, m=P),
            w4_sc_raw[:].rearrange("p a (b m t) -> p (a b) t m", t=PACK, m=P),
        )
        deal_w4(0)
        v2_sc = held([P, S2], U8, "v2_sc")
        nc.vector.tensor_copy(v2_sc[:], tab2_sc[:].indirect(idx2[:]))
        gather_v(1, 0)
        gather_v(1, 1)
        tab2 = held([P, 2 * T3], I32, "tab1")
        for b in range(2):
            nc.sync.dma_start(tab2[:, b * T3 : (b + 1) * T3], words(tab2_words, b))
        quantise_w1(1, 0, calls=2)

        h_q, h_sc, h_bf, h_two = {}, {}, {}, {}
        for b in range(2):
            for half in range(2):
                h_sc[b, half] = held([P, BANK], U8, "h_sc%d%d" % (b, half))
        for u in (0, 2, 4):
            h_two[u] = held([P, 2 * UNIT * PACK], BF16, "h_bf%d" % u)
            h_bf[u] = h_two[u][:, : UNIT * PACK]
            h_bf[u + 1] = h_two[u][:, UNIT * PACK :]
        for u in (6, 7):
            single = held([P, UNIT * PACK], BF16, "h_bf%d" % u)
            h_bf[u] = single[:]
        for half in range(2):
            h_q[1, half] = held([P, BANK], U32, "h_q1%d" % half)

        def quantise_h(b, half, lo, hi, src):
            nc.vector.quantize_mx(h_q[b, half][:, lo:hi].bitcast(FP8X4), h_sc[b, half][:, lo:hi], src)

        squared, linear = {}, {}

        def open_unit(u):
            base = 4 * (u % 2)
            squared[u] = [bank(base), bank(base + 1)]
            linear[u] = [bank(base + 2), bank(base + 3)]

        def guests(u):
            b, quarter = divmod(u, S // UNIT)
            half, c0 = divmod(quarter * UNIT, BANK)
            return b, half, c0, quarter * UNIT

        def w1_pass(u, pair, a):
            b, half, c0, j0 = guests(u)
            for s in range(2):
                t = 2 * pair + s
                nc.tensor.matmul_mx(
                    squared[u][pair][:, s * UNIT : (s + 1) * UNIT],
                    lhsT=w1_q[a, b][:, t * P : (t + 1) * P].bitcast(FP8X4),
                    lhsT_scale=w1_sc[a, b][:, t * P : (t + 1) * P],
                    rhs=v[a, half][:, c0 : c0 + UNIT].bitcast(FP8X4),
                    rhs_scale=v_sc[a][:, j0 : j0 + UNIT],
                    start=(a == 0 and s == 0),
                    stop=(a == 1 and s == 1),
                )

        def w4_pass(u, g, a):
            b, half, c0, j0 = guests(u)
            for t in range(PACK):
                sc0 = (2 * a + b) * KP + t * P
                nc.tensor.matmul_mx(
                    linear[u][g][:, t * P : (t + 1) * P],
                    lhsT=w4_q[b][:, a, 2 * t * P : 2 * (t + 1) * P].bitcast(FP4X4),
                    lhsT_scale=w4_sc[:, sc0 : sc0 + P],
                    rhs=v[a, half][:, c0 + g * P : c0 + (g + 1) * P].bitcast(FP8X4),
                    rhs_scale=v_sc[a][:, j0 + g * P : j0 + (g + 1) * P],
                    start=(a == 0 and t == 0),
                    stop=(a == 1 and t == PACK - 1),
                )

        def close_unit(u):
            sq = ring.tile([P, 2, UNIT, 2], F32, name="sq", align_bytes=64)
            for pair in range(2):
                nc.scalar.activation(sq[:, pair], squared[u][pair][:].rearrange("p (s j) -> p j s", s=2), ACT.Square)
            for g in range(2):
                nc.vector.tensor_tensor(
                    h_bf[u][:, g * BANK : (g + 1) * BANK].rearrange("p (j r s) -> p j r s", r=2, s=2),
                    linear[u][g][:].rearrange("p (r s j) -> p j r s", r=2, s=2),
                    sq[:, :, g * P : (g + 1) * P, :].rearrange("p r j s -> p j r s"),
                    ALU.subtract,
                )

        def whole_unit(u):
            open_unit(u)
            for one_pass in (w1_pass, w4_pass):
                for i in range(2):
                    for a in range(2):
                        one_pass(u, i, a)
            close_unit(u)

        v2 = {}

        def gather_v2(part, name):
            cols = slice(part * S2 // 2 // PER_COL, (part + 1) * S2 // 2 // PER_COL)
            v2[part] = held([P, 2, S2 // 2], U32, name)
            for b in range(2):
                nc.vector.tensor_copy(v2[part][:, b, :], tab2[:, b * T3 : (b + 1) * T3].bitcast(U32).indirect(idx2[:, cols]))

        for u in (0, 1):
            open_unit(u)
        for one_pass, a in ((w1_pass, 0), (w4_pass, 0), (w4_pass, 1)):
            for u in (0, 1):
                for i in range(2):
                    one_pass(u, i, a)
        for u in (0, 1):
            for i in range(2):
                w1_pass(u, i, 1)
            close_unit(u)
        whole_unit(2)
        whole_unit(3)
        deal_w4(1)
        quantise_w1(0, 1, calls=1)
        allow_sb = staging()
        nc.sync.dma_start(allow_sb[:], allow.rearrange("(m p) n -> p m n", p=P))
        quantise_w1(1, 1, calls=1)
        for half in range(2):
            h_q[0, half] = ring.tile([P, BANK], U32, name="w1_bf", align_bytes=64)
        open_unit(4)
        for i in range(2):
            for a in range(2):
                w4_pass(4, i, a)
        for a in range(2):
            for i in range(2):
                w1_pass(4, i, a)
        close_unit(4)
        quantise_h(0, 0, 0, BANK, h_two[0][:])
        whole_unit(5)
        quantise_h(0, 1, 0, BANK, h_two[2][:])
        gather_v2(0, "v2_early")
        whole_unit(6)
        quantise_h(1, 0, 0, BANK, h_two[4][:])
        quantise_h(1, 1, 0, UNIT, h_bf[6])
        whole_unit(7)
        for g in range(2):
            quantise_h(1, 1, UNIT + g * P, UNIT + (g + 1) * P, h_bf[7][:, g * BANK : (g + 1) * BANK])
        gather_v2(1, "h_bf7")

        e = [held([P, S], F32, "e%d" % m) for m in range(S2 // P)]

        def scores(m, where, half, lo, hi, pieces):
            acc = bank(where)
            for i, (b, c0, c1) in enumerate(pieces):
                nc.tensor.matmul_mx(
                    acc[:, c0:c1],
                    lhsT=v2[m // 2][:, b, (m % 2) * P : (m % 2 + 1) * P].bitcast(FP8X4),
                    lhsT_scale=v2_sc[THEME_ROW + 4 * b : P, m * P : (m + 1) * P],
                    rhs=h_q[b, half][:, c0:c1].bitcast(FP8X4),
                    rhs_scale=h_sc[b, half][:, c0:c1],
                    start=(i == 0),
                    stop=(i == len(pieces) - 1),
                )
            nc.scalar.copy(e[m][:, half * BANK + lo : half * BANK + hi], acc[:, lo:hi])

        whole = [(0, 0, BANK), (1, 0, BANK)]
        cut = UNIT + P
        scores(0, 0, 0, 0, BANK, whole)
        scores(0, 4, 1, 0, cut, [(b, c0, c1) for b in range(2) for c0, c1 in ((0, UNIT), (UNIT, cut))])
        scores(0, 5, 1, cut, BANK, [(b, cut, BANK) for b in range(2)])
        scores(1, 1, 0, 0, BANK, whole)
        scores(1, 6, 1, 0, BANK, [(0, 0, BANK), (1, 0, UNIT), (1, UNIT, cut), (1, cut, BANK)])
        for m, second_bank in ((2, 7), (3, 0)):
            scores(m, m, 0, 0, BANK, whole)
            scores(m, second_bank, 1, 0, BANK, whole)

        guest, agree = {}, {}

        def pick_guest(m):
            guest[m] = held([P, PAIRS], F32, "guest%d" % m)
            nc.vector.tensor_copy(guest[m][:], e[m][:].indirect(p1[:]))

        def compare(m, lo, hi):
            gap = held([P, hi - lo], F32, "gap%d_%d" % (m, lo))
            nc.vector.tensor_tensor(
                gap[:], e[m][:].indirect(p2[:, lo // PER_COL : hi // PER_COL]), guest[m][:, lo:hi], ALU.subtract
            )
            dist = held([P, hi - lo], F32, "dist%d_%d" % (m, lo))
            nc.scalar.activation(dist[:], gap[:], ACT.Abs)
            agree[m, lo] = held([P, hi - lo], F32, "agree%d_%d" % (m, lo))
            nc.scalar.activation(agree[m, lo][:], dist[:], ACT.Exp, scale=-1.0)

        def finish(m, lo, hi):
            res = held([P, hi - lo], F32, "res%d_%d" % (m, lo))
            nc.vector.tensor_tensor(res[:], agree[m, lo][:], allow_sb[:, m, lo:hi], ALU.mult)
            nc.sync.dma_start(out[m * P : (m + 1) * P, lo:hi], res[:])

        pick_guest(0)
        pick_guest(1)
        compare(0, 0, PAIRS)
        pick_guest(2)
        compare(1, 0, PAIRS)
        finish(0, 0, PAIRS)
        pick_guest(3)
        compare(2, 0, PAIRS)
        finish(1, 0, PAIRS)
        compare(3, 0, PAIRS // 2)
        compare(3, PAIRS // 2, PAIRS)
        finish(2, 0, PAIRS)
        finish(3, 0, PAIRS // 2)
        finish(3, PAIRS // 2, PAIRS)
